import numpy as np
import ml_dtypes


def mxq(x, axis, fmt="e4m3"):
    dtype, down = {"e4m3": (ml_dtypes.float8_e4m3fn, 7), "e5m2": (ml_dtypes.float8_e5m2, 14)}[fmt]
    v = np.moveaxis(np.asarray(x, np.float32).astype(ml_dtypes.bfloat16).astype(np.float64), axis, -1)
    blocks = v.reshape(v.shape[:-1] + (-1, 32))
    amax = np.abs(blocks).max(-1, keepdims=True)
    byte = np.maximum(np.where(amax > 0, np.frexp(amax)[1] - 1 + 127, 0) - down, 1)
    scale = np.exp2(byte - 127.0)
    codes = (blocks / scale).astype(np.float32).astype(dtype).astype(np.float64)
    return np.moveaxis((codes * scale).reshape(v.shape), -1, axis)


WIDE = False


def mx_kscale(k):
    if not WIDE:
        return np.ones(k)
    levels = np.array([10, -10, 5, -5, 0])
    if k % 512:
        return np.exp2(np.random.permutation(np.resize(levels, k // 32))).repeat(32)
    a = np.empty((k // 512, 16))
    for p in range(k // 512):
        a[p, :8] = np.random.permutation(np.resize(levels, 8))
        for g in range(8):
            far = levels[np.abs(levels - a[p, g]) >= 10]
            a[p, g + 8] = far[np.random.randint(len(far))]
    return np.exp2(a.ravel()).repeat(32)


def f64(x):
    return np.asarray(x).astype(np.float64)


def striped(idx):
    return np.tile(idx.reshape(-1, 16).T, (8, 1)).astype(np.uint16)


def unstriped(offs):
    return offs[:16].T.reshape(-1).astype(np.int64)


def pack_weight(w):
    k, n = w.shape
    w = f64(np.asarray(w, np.float32).astype(ml_dtypes.bfloat16)).reshape(k // 32, 32, n)
    amax = np.abs(w).max(1)
    byte = np.clip(np.where(amax > 0, np.frexp(amax)[1] - 1 + 127 - 7, 1), 1, 254)
    scaled = (w * np.exp2(127.0 - byte)[:, None, :]).reshape(k, n).astype(np.float32)
    words = np.ascontiguousarray(scaled.reshape(k // 512, 128, 4, n).transpose(0, 1, 3, 2)).astype(ml_dtypes.float8_e4m3fn).view(np.uint8)
    return words, np.ascontiguousarray(byte.astype(np.uint8).reshape(k // 512, 16, n))


def unpack_weight(words, scales):
    g, p, n, _ = words.shape
    vals = np.ascontiguousarray(words).view(ml_dtypes.float8_e4m3fn).astype(np.float64) * np.repeat(np.exp2(scales.astype(np.float64) - 127.0), 8, axis=1)[..., None]
    return vals.transpose(0, 1, 3, 2).reshape(g * 512, n)


def relu(v):
    return np.maximum(v, 0.0)


K, T, S, H, V, W = 512, 1024, 512, 512, 512, 2048
P = 2 ** 7


def setup_inputs():
    n = np.random.standard_normal
    s = mx_kscale(K)[:, None]
    u = mx_kscale(H)
    packed_xT = pack_weight(n((K, T)) * s)
    packed_eT = pack_weight(n((H, W)) / np.sqrt(H) / u[:, None])
    return {
        "x_words": packed_xT[0],
        "x_scales": packed_xT[1],
        "w1": (n((K, H)) / np.sqrt(K) / s * u).astype(np.float32),
        "e_words": packed_eT[0],
        "e_scales": packed_eT[1],
        "own": (np.random.uniform(0.8, 1.6, (S, 1))).astype(np.float32),
        "inv": (np.random.uniform(0.6, 1.2, (S, 1))).astype(np.float32),
        "qn": (np.tile(np.random.uniform(0.8, 1.6, W), (P, 1))).astype(np.float32),
        "offs": striped(np.random.permutation(T)[:S]),
        "code": striped(np.random.permutation(W)[:V]),
    }


def reference(x_words, x_scales, w1, e_words, e_scales, own, inv, qn, offs, code):
    xq = unpack_weight(x_words, x_scales)[:, unstriped(offs)]
    h = mxq(f64(w1), 0, "e4m3").T @ xq
    e_code = unpack_weight(e_words, e_scales)[:, unstriped(code)]
    y = 0.4 * ((mxq(h, 0, "e4m3").T @ e_code))
    rr = -1.0 * y + f64(own)
    par = f64(inv) * ((rr) ** 2)
    tot = rr - y + f64(qn)[:1][:, unstriped(code)]
    l = 3.0 * par + relu(tot - par)
    ww = -2.0 * l
    ex = np.exp(ww - ww.max(axis=1, keepdims=True))
    return ex / ex.sum(axis=1, keepdims=True)

@@ -1,0 +1,210 @@
+from contextlib import ExitStack
+
+import concourse.mybir as mybir
+from concourse.masks import make_identity
+
+K, T, S, H, V, W = 512, 1024, 512, 512, 512, 2048
+P = 128
+PACK = 4
+BLOCKS = S // P
+
+FLOPS = 2 * K * H * S + 2 * H * S * V
+BYTES = K * T + 16 * T + 4 * K * H + H * W + 16 * W + 8 * S + 4 * W + 2 * 2 * P * 32 + 4 * S * V
+
+F32 = mybir.dt.float32
+BF16 = mybir.dt.bfloat16
+I32 = mybir.dt.int32
+U32 = mybir.dt.uint32
+U16 = mybir.dt.uint16
+U8 = mybir.dt.uint8
+FP8X4 = mybir.dt.float8_e4m3fn_x4
+ALU = mybir.AluOpType
+ACT = mybir.ActivationFunctionType
+AXIS = mybir.AxisListType
+
+
+def tile_picked_yscann_soft_p_kernel(
+    tc, x_words, x_scales, w1, e_words, e_scales, own, inv, qn, offs, code, out
+):
+    nc = tc.nc
+    with ExitStack() as ctx:
+        keep = ctx.enter_context(tc.tile_pool(name="keep", bufs=1))
+        psum = ctx.enter_context(tc.psum_pool(name="psum", bufs=1))
+
+        offs_sb = keep.tile([P, S // 16], U16, name="offs_sb")
+        code_sb = keep.tile([P, V // 16], U16, name="code_sb")
+        xw_all = keep.tile([P, T], I32, name="xw_all")
+        xs_all = keep.tile([P, T], U8, name="xs_all")
+        ew_all = keep.tile([P, W], I32, name="ew_all")
+        es_all = keep.tile([P, W], U8, name="es_all")
+        q_all = keep.tile([P, W], F32, name="q_all")
+        w_raw = keep.tile([P, PACK, H], F32, name="w_raw")
+        rows = keep.tile([P, P], F32, name="rows")
+        ident = keep.tile([P, P], F32, name="ident")
+        warm = keep.tile([P, 1], F32, name="warm")
+
+        nc.vector.memset(q_all[:].bitcast(I32), 0)
+        nc.gpsimd.memset(rows[:], 0.0)
+        nc.scalar.activation(out=warm[:], in_=rows[:, 0:1], func=ACT.Exp)
+
+        def load_scales(tile, scales):
+            for q in range(4):
+                nc.sync.dma_start(
+                    out=tile[32 * q : 32 * q + 32, :].bitcast(I32),
+                    in_=scales[0, 4 * q : 4 * q + 4, :].bitcast(I32).partition_broadcast(8),
+                )
+
+        w_view = w1.rearrange("(p j) c -> p j c", j=PACK)
+        nc.gpsimd.dma_start(out=rows[0:BLOCKS, :], in_=own.rearrange("(b p) o -> b (p o)", p=P))
+        nc.gpsimd.dma_start(out=rows[BLOCKS : 2 * BLOCKS, :], in_=inv.rearrange("(b p) o -> b (p o)", p=P))
+        make_identity(nc, ident[:])
+        nc.sync.dma_start(offs_sb[:], offs)
+        nc.sync.dma_start(code_sb[:], code)
+        load_scales(xs_all, x_scales)
+        nc.sync.dma_start(out=xw_all[:], in_=x_words[0].rearrange("p n t -> p (n t)").bitcast(I32))
+        nc.sync.dma_start(out=w_raw[:], in_=w_view)
+        nc.scalar.dma_start(out=q_all[0:1, :], in_=qn[0:1, :])
+        load_scales(es_all, e_scales)
+        nc.sync.dma_start(out=ew_all[:], in_=e_words[0].rearrange("p n t -> p (n t)").bitcast(I32))
+
+        xw = keep.tile([P, S], U32, name="xw", align_bytes=64)
+        xs = keep.tile([P, S], U8, name="xs", align_bytes=64)
+        ew = keep.tile([P, V], U32, name="ew", align_bytes=64)
+        es = keep.tile([P, V], U8, name="es", align_bytes=64)
+        q_row = keep.tile([P, V], F32, name="q_row")
+
+        nc.vector.tensor_copy(xs[:], xs_all[:].indirect(offs_sb[:]))
+        nc.vector.tensor_copy(xw[:], xw_all[:].bitcast(U32).indirect(offs_sb[:]))
+        nc.vector.tensor_copy(q_row[:], q_all[:].indirect(code_sb[:]))
+
+        turn = psum.tile([P, PACK, P], F32, name="turn", tag="turn")
+        nc.tensor.transpose(turn[:, 0, :], rows[:], ident[:])
+        once = keep.tile([P, 2 * BLOCKS], F32, name="once")
+        twice = keep.tile([P, 2 * BLOCKS], F32, name="twice")
+        halved = keep.tile([P, BLOCKS], F32, name="halved")
+        nc.scalar.copy(out=once[:], in_=turn[:, 0, 0 : 2 * BLOCKS])
+        nc.gpsimd.tensor_scalar(
+            out=twice[:], in0=once[:], scalar1=2.0, scalar2=1.0, op0=ALU.mult, op1=ALU.mult
+        )
+        nc.gpsimd.tensor_scalar(
+            out=halved[:], in0=once[:, BLOCKS:], scalar1=0.5, scalar2=1.0, op0=ALU.mult, op1=ALU.mult
+        )
+
+        w_bf = keep.tile([P, PACK * H], BF16, name="w_bf", align_bytes=64)
+        w_dst = w_bf[:].rearrange("p (t m j) -> p m j t", t=PACK, j=PACK)
+        w_src = w_raw[:].rearrange("p j (m t) -> p m j t", t=PACK)
+        half = H // PACK // 2
+        nc.scalar.copy(out=w_dst[:, :half], in_=w_src[:, :half])
+        nc.vector.tensor_copy(out=w_dst[:, half:], in_=w_src[:, half:])
+        nc.vector.tensor_copy(es[:], es_all[:].indirect(code_sb[:]))
+        wq = keep.tile([P, H], U32, name="wq", align_bytes=64)
+        ws = keep.tile([P, H], U8, name="ws", align_bytes=64)
+        nc.vector.quantize_mx(out=wq[:].bitcast(FP8X4), scales=ws[:], in_=w_bf[:])
+        nc.vector.tensor_copy(ew[:], ew_all[:].bitcast(U32).indirect(code_sb[:]))
+
+        turn_q = psum.tile([P, PACK, P], F32, name="turn_q", tag="turn")
+        for c in range(PACK):
+            nc.tensor.transpose(turn_q[:, c, :], q_row[:, c * P : (c + 1) * P], ident[:])
+        q_col = keep.tile([P, PACK], F32, name="q_col")
+        nc.scalar.copy(out=q_col[:], in_=turn_q[:, :, 0])
+        q_bank = psum.tile([P, V], F32, name="q_bank", tag="q_bank")
+        for c in range(PACK):
+            nc.tensor.transpose(
+                q_bank[:, c * P : (c + 1) * P], q_col[:, c : c + 1].to_broadcast([P, P]), ident[:]
+            )
+
+        hq = []
+        hs = []
+        qo = []
+        for b in range(BLOCKS):
+            cols = slice(b * P, (b + 1) * P)
+            qo_b = keep.tile([P, V], F32, name=f"qo{b}")
+            nc.scalar.activation(
+                out=qo_b[:], in_=q_bank[:], func=ACT.Identity, scale=2.0, bias=twice[:, b : b + 1]
+            )
+            qo.append(qo_b)
+            h_bank = psum.tile([P, PACK, P], F32, name="h_bank", tag="h_bank", bufs=2)
+            for t in range(PACK):
+                nc.tensor.matmul_mx(
+                    out=h_bank[:, t, :],
+                    lhsT=wq[:, t * P : (t + 1) * P].bitcast(FP8X4),
+                    lhsT_scale=ws[:, t * P : (t + 1) * P],
+                    rhs=xw[:, cols].bitcast(FP8X4),
+                    rhs_scale=xs[:, cols],
+                    start=True,
+                    stop=True,
+                )
+            h_bf = keep.tile([P, P, PACK], BF16, name=f"h_bf{b}", align_bytes=64)
+            nc.scalar.copy(out=h_bf[:], in_=h_bank[:].rearrange("p t n -> p n t"))
+            hq_b = keep.tile([P, P], U32, name=f"hq{b}", align_bytes=64)
+            hs_b = keep.tile([P, P], U8, name=f"hs{b}", align_bytes=64)
+            nc.vector.quantize_mx(
+                out=hq_b[:].bitcast(FP8X4), scales=hs_b[:], in_=h_bf[:].rearrange("p n t -> p (n t)")
+            )
+            hq.append(hq_b)
+            hs.append(hs_b)
+
+        def stage_tiles(name, width):
+            return [keep.tile([P, width], F32, name=f"{name}{b}") for b in range(BLOCKS)]
+
+        tot2, rr_sq, big2, cost2, ex, res = (
+            stage_tiles(n, V) for n in ("tot2", "rr_sq", "big2", "cost2", "ex", "res")
+        )
+        least, total, share = (stage_tiles(n, 1) for n in ("least", "total", "share"))
+        z = [psum.tile([P, V], F32, name=f"z{b}", tag=f"z{b}") for b in range(BLOCKS)]
+
+        def product(b):
+            nc.tensor.matmul_mx(
+                out=z[b][:],
+                lhsT=hq[b][:].bitcast(FP8X4),
+                lhsT_scale=hs[b][:],
+                rhs=ew[:].bitcast(FP8X4),
+                rhs_scale=es[:],
+                start=True,
+                stop=True,
+            )
+
+        def read_bank(b):
+            nc.vector.scalar_tensor_tensor(
+                out=tot2[b][:], in0=z[b][:], scalar=-1.6, in1=qo[b][:], op0=ALU.mult, op1=ALU.add
+            )
+            nc.scalar.activation(
+                out=rr_sq[b][:], in_=z[b][:], func=ACT.Square, scale=-0.8, bias=twice[:, b : b + 1]
+            )
+
+        def larger(b):
+            nc.vector.scalar_tensor_tensor(
+                out=big2[b][:], in0=rr_sq[b][:], scalar=halved[:, b : b + 1], in1=tot2[b][:],
+                op0=ALU.mult, op1=ALU.max,
+            )
+
+        def cost(b):
+            nc.vector.scalar_tensor_tensor(
+                out=cost2[b][:], in0=rr_sq[b][:], scalar=once[:, BLOCKS + b : BLOCKS + b + 1], in1=big2[b][:],
+                op0=ALU.mult, op1=ALU.add,
+            )
+
+        def smallest(b):
+            nc.vector.tensor_reduce(out=least[b][:], in_=cost2[b][:], axis=AXIS.X, op=ALU.min)
+            nc.scalar.activation(
+                out=ex[b][:], in_=cost2[b][:], func=ACT.Exp, scale=-1.0, bias=least[b][:],
+                accum_out=total[b][:],
+            )
+
+        def finish(b):
+            nc.vector.reciprocal(out=share[b][:], in_=total[b][:])
+            if b < BLOCKS - 1:
+                nc.scalar.activation(out=res[b][:], in_=ex[b][:], func=ACT.Copy, scale=share[b][:])
+            else:
+                nc.vector.tensor_scalar(
+                    out=res[b][:], in0=ex[b][:], scalar1=share[b][:], scalar2=None, op0=ALU.mult
+                )
+            nc.sync.dma_start(out=out[b * P : (b + 1) * P, :], in_=res[b][:])
+
+        for b in range(BLOCKS):
+            product(b)
+        stages = (read_bank, larger, cost, smallest, finish)
+        for step in range(BLOCKS + len(stages) - 1):
+            for k in reversed(range(len(stages))):
+                if 0 <= step - k < BLOCKS:
+                    stages[k](step - k)

@@ -7,6 +7,8 @@ K, T, S, H, V, W = 512, 1024, 512, 512, 512, 2048
 P = 128
 PACK = 4
 BLOCKS = S // P
+SCALAR_SHARE = 80
+ROW0 = P - 2 * BLOCKS
 
 FLOPS = 2 * K * H * S + 2 * H * S * V
 BYTES = K * T + 16 * T + 4 * K * H + H * W + 16 * W + 8 * S + 4 * W + 2 * 2 * P * 32 + 4 * S * V
@@ -34,18 +36,18 @@ def tile_picked_yscann_soft_p_kernel(
         offs_sb = keep.tile([P, S // 16], U16, name="offs_sb")
         code_sb = keep.tile([P, V // 16], U16, name="code_sb")
         xw_all = keep.tile([P, T], I32, name="xw_all")
-        xs_all = keep.tile([P, T], U8, name="xs_all")
-        ew_all = keep.tile([P, W], I32, name="ew_all")
-        es_all = keep.tile([P, W], U8, name="es_all")
-        q_all = keep.tile([P, W], F32, name="q_all")
+        xs_all = keep.tile([P, T], U8, name="xs_all", tag="e_words", align_bytes=64)
+        ew_all = keep.tile([P, W], I32, name="ew_all", tag="e_words", align_bytes=64)
+        es_all = keep.tile([P, W], U8, name="es_all", tag="e_scales", align_bytes=64)
+        q_all = keep.tile([P, W], F32, name="q_all", tag="norms", align_bytes=64)
         w_raw = keep.tile([P, PACK, H], F32, name="w_raw")
         rows = keep.tile([P, P], F32, name="rows")
         ident = keep.tile([P, P], F32, name="ident")
         warm = keep.tile([P, 1], F32, name="warm")
 
-        nc.vector.memset(q_all[:].bitcast(I32), 0)
-        nc.gpsimd.memset(rows[:], 0.0)
-        nc.scalar.activation(out=warm[:], in_=rows[:, 0:1], func=ACT.Exp)
+        nc.vector.memset(q_all[: P - 1, :], 0.0)
+        nc.gpsimd.memset(rows[:ROW0, :], 0.0)
+        nc.scalar.activation(out=warm[:32, :], in_=rows[:32, 0:1], func=ACT.Exp)
 
         def load_scales(tile, scales):
             for q in range(4):
@@ -55,75 +57,67 @@ def tile_picked_yscann_soft_p_kernel(
                 )
 
         w_view = w1.rearrange("(p j) c -> p j c", j=PACK)
-        nc.gpsimd.dma_start(out=rows[0:BLOCKS, :], in_=own.rearrange("(b p) o -> b (p o)", p=P))
-        nc.gpsimd.dma_start(out=rows[BLOCKS : 2 * BLOCKS, :], in_=inv.rearrange("(b p) o -> b (p o)", p=P))
+        nc.gpsimd.dma_start(out=rows[ROW0 : ROW0 + BLOCKS, :], in_=own.rearrange("(b p) o -> b (p o)", p=P))
+        nc.gpsimd.dma_start(out=rows[ROW0 + BLOCKS :, :], in_=inv.rearrange("(b p) o -> b (p o)", p=P))
         make_identity(nc, ident[:])
         nc.sync.dma_start(offs_sb[:], offs)
         nc.sync.dma_start(code_sb[:], code)
         load_scales(xs_all, x_scales)
         nc.sync.dma_start(out=xw_all[:], in_=x_words[0].rearrange("p n t -> p (n t)").bitcast(I32))
         nc.sync.dma_start(out=w_raw[:], in_=w_view)
-        nc.scalar.dma_start(out=q_all[0:1, :], in_=qn[0:1, :])
+        nc.sync.dma_start(out=q_all[P - 1 :, :], in_=qn[0:1, :])
         load_scales(es_all, e_scales)
         nc.sync.dma_start(out=ew_all[:], in_=e_words[0].rearrange("p n t -> p (n t)").bitcast(I32))
 
         xw = keep.tile([P, S], U32, name="xw", align_bytes=64)
         xs = keep.tile([P, S], U8, name="xs", align_bytes=64)
-        ew = keep.tile([P, V], U32, name="ew", align_bytes=64)
-        es = keep.tile([P, V], U8, name="es", align_bytes=64)
+        ew = keep.tile([P, V], U32, name="ew", tag="e_scales", align_bytes=64)
+        es = keep.tile([P, V], U8, name="es", tag="w_bf", align_bytes=64)
         q_row = keep.tile([P, V], F32, name="q_row")
 
         nc.vector.tensor_copy(xs[:], xs_all[:].indirect(offs_sb[:]))
         nc.vector.tensor_copy(xw[:], xw_all[:].bitcast(U32).indirect(offs_sb[:]))
         nc.vector.tensor_copy(q_row[:], q_all[:].indirect(code_sb[:]))
 
-        turn = psum.tile([P, PACK, P], F32, name="turn", tag="turn")
+        turn = psum.tile([P, PACK, P], F32, name="turn", tag="z3")
         nc.tensor.transpose(turn[:, 0, :], rows[:], ident[:])
-        once = keep.tile([P, 2 * BLOCKS], F32, name="once")
-        twice = keep.tile([P, 2 * BLOCKS], F32, name="twice")
-        halved = keep.tile([P, BLOCKS], F32, name="halved")
-        nc.scalar.copy(out=once[:], in_=turn[:, 0, 0 : 2 * BLOCKS])
-        nc.gpsimd.tensor_scalar(
-            out=twice[:], in0=once[:], scalar1=2.0, scalar2=1.0, op0=ALU.mult, op1=ALU.mult
-        )
-        nc.gpsimd.tensor_scalar(
-            out=halved[:], in0=once[:, BLOCKS:], scalar1=0.5, scalar2=1.0, op0=ALU.mult, op1=ALU.mult
-        )
+        own_s = keep.tile([P, BLOCKS], F32, name="own_s")
+        inv_a = keep.tile([P, BLOCKS], F32, name="inv_a")
+        inv_b = keep.tile([P, BLOCKS], F32, name="inv_b")
+        nc.scalar.activation(out=own_s[:], in_=turn[:, 0, ROW0 : ROW0 + BLOCKS], func=ACT.Copy, scale=-1.25)
+        nc.scalar.activation(out=inv_a[:], in_=turn[:, 0, ROW0 + BLOCKS :], func=ACT.Copy, scale=-0.8)
+        nc.scalar.activation(out=inv_b[:], in_=turn[:, 0, ROW0 + BLOCKS :], func=ACT.Copy, scale=-1.6)
 
-        w_bf = keep.tile([P, PACK * H], BF16, name="w_bf", align_bytes=64)
+        w_bf = keep.tile([P, PACK * H], BF16, name="w_bf", tag="w_bf", align_bytes=64)
         w_dst = w_bf[:].rearrange("p (t m j) -> p m j t", t=PACK, j=PACK)
         w_src = w_raw[:].rearrange("p j (m t) -> p m j t", t=PACK)
-        half = H // PACK // 2
-        nc.scalar.copy(out=w_dst[:, :half], in_=w_src[:, :half])
-        nc.vector.tensor_copy(out=w_dst[:, half:], in_=w_src[:, half:])
-        nc.vector.tensor_copy(es[:], es_all[:].indirect(code_sb[:]))
-        wq = keep.tile([P, H], U32, name="wq", align_bytes=64)
+        nc.scalar.copy(out=w_dst[:, :SCALAR_SHARE], in_=w_src[:, :SCALAR_SHARE])
+        nc.vector.tensor_copy(out=w_dst[:, SCALAR_SHARE:], in_=w_src[:, SCALAR_SHARE:])
+        wq = keep.tile([P, H], U32, name="wq", tag="norms", align_bytes=64)
         ws = keep.tile([P, H], U8, name="ws", align_bytes=64)
         nc.vector.quantize_mx(out=wq[:].bitcast(FP8X4), scales=ws[:], in_=w_bf[:])
+        nc.vector.tensor_copy(es[:], es_all[:].indirect(code_sb[:]))
         nc.vector.tensor_copy(ew[:], ew_all[:].bitcast(U32).indirect(code_sb[:]))
 
-        turn_q = psum.tile([P, PACK, P], F32, name="turn_q", tag="turn")
+        turn_q = psum.tile([P, PACK, P], F32, name="turn_q", tag="z2")
         for c in range(PACK):
             nc.tensor.transpose(turn_q[:, c, :], q_row[:, c * P : (c + 1) * P], ident[:])
         q_col = keep.tile([P, PACK], F32, name="q_col")
-        nc.scalar.copy(out=q_col[:], in_=turn_q[:, :, 0])
-        q_bank = psum.tile([P, V], F32, name="q_bank", tag="q_bank")
+        nc.scalar.copy(out=q_col[:], in_=turn_q[:, :, P - 1])
+        q_bank = psum.tile([P, V], F32, name="q_bank", tag="z1")
         for c in range(PACK):
             nc.tensor.transpose(
                 q_bank[:, c * P : (c + 1) * P], q_col[:, c : c + 1].to_broadcast([P, P]), ident[:]
             )
+        q_s = keep.tile([P, V], F32, name="q_s")
+        nc.scalar.activation(out=q_s[:], in_=q_bank[:], func=ACT.Copy, scale=-1.25)
 
+        hq_all = keep.tile([P, S], U32, name="hq_all", tag="e_words", align_bytes=64)
         hq = []
         hs = []
-        qo = []
         for b in range(BLOCKS):
             cols = slice(b * P, (b + 1) * P)
-            qo_b = keep.tile([P, V], F32, name=f"qo{b}")
-            nc.scalar.activation(
-                out=qo_b[:], in_=q_bank[:], func=ACT.Identity, scale=2.0, bias=twice[:, b : b + 1]
-            )
-            qo.append(qo_b)
-            h_bank = psum.tile([P, PACK, P], F32, name="h_bank", tag="h_bank", bufs=2)
+            h_bank = psum.tile([P, PACK, P], F32, name="h_bank", tag="h_bank", bufs=4)
             for t in range(PACK):
                 nc.tensor.matmul_mx(
                     out=h_bank[:, t, :],
@@ -136,10 +130,10 @@ def tile_picked_yscann_soft_p_kernel(
                 )
             h_bf = keep.tile([P, P, PACK], BF16, name=f"h_bf{b}", align_bytes=64)
             nc.scalar.copy(out=h_bf[:], in_=h_bank[:].rearrange("p t n -> p n t"))
-            hq_b = keep.tile([P, P], U32, name=f"hq{b}", align_bytes=64)
+            hq_b = hq_all[:, cols]
             hs_b = keep.tile([P, P], U8, name=f"hs{b}", align_bytes=64)
             nc.vector.quantize_mx(
-                out=hq_b[:].bitcast(FP8X4), scales=hs_b[:], in_=h_bf[:].rearrange("p n t -> p (n t)")
+                out=hq_b.bitcast(FP8X4), scales=hs_b[:], in_=h_bf[:].rearrange("p n t -> p (n t)")
             )
             hq.append(hq_b)
             hs.append(hs_b)
@@ -156,7 +150,7 @@ def tile_picked_yscann_soft_p_kernel(
         def product(b):
             nc.tensor.matmul_mx(
                 out=z[b][:],
-                lhsT=hq[b][:].bitcast(FP8X4),
+                lhsT=hq[b].bitcast(FP8X4),
                 lhsT_scale=hs[b][:],
                 rhs=ew[:].bitcast(FP8X4),
                 rhs_scale=es[:],
@@ -166,28 +160,32 @@ def tile_picked_yscann_soft_p_kernel(
 
         def read_bank(b):
             nc.vector.scalar_tensor_tensor(
-                out=tot2[b][:], in0=z[b][:], scalar=-1.6, in1=qo[b][:], op0=ALU.mult, op1=ALU.add
+                out=tot2[b][:], in0=z[b][:], scalar=own_s[:, b : b + 1], in1=q_s[:], op0=ALU.add, op1=ALU.add
             )
             nc.scalar.activation(
-                out=rr_sq[b][:], in_=z[b][:], func=ACT.Square, scale=-0.8, bias=twice[:, b : b + 1]
+                out=rr_sq[b][:], in_=z[b][:], func=ACT.Square, scale=0.5, bias=own_s[:, b : b + 1]
             )
+
 
         def larger(b):
             nc.vector.scalar_tensor_tensor(
-                out=big2[b][:], in0=rr_sq[b][:], scalar=halved[:, b : b + 1], in1=tot2[b][:],
-                op0=ALU.mult, op1=ALU.max,
+                out=big2[b][:], in0=rr_sq[b][:], scalar=inv_a[:, b : b + 1], in1=tot2[b][:],
+                op0=ALU.mult, op1=ALU.min,
             )
 
         def cost(b):
             nc.vector.scalar_tensor_tensor(
-                out=cost2[b][:], in0=rr_sq[b][:], scalar=once[:, BLOCKS + b : BLOCKS + b + 1], in1=big2[b][:],
+                out=cost2[b][:], in0=rr_sq[b][:], scalar=inv_b[:, b : b + 1], in1=big2[b][:],
                 op0=ALU.mult, op1=ALU.add,
             )
 
         def smallest(b):
-            nc.vector.tensor_reduce(out=least[b][:], in_=cost2[b][:], axis=AXIS.X, op=ALU.min)
+            nc.vector.tensor_scalar(
+                out=big2[b][:], in0=cost2[b][:], scalar1=-1.6, scalar2=None, op0=ALU.mult, op1=ALU.min,
+                accum_out=least[b][:],
+            )
             nc.scalar.activation(
-                out=ex[b][:], in_=cost2[b][:], func=ACT.Exp, scale=-1.0, bias=least[b][:],
+                out=ex[b][:], in_=big2[b][:], func=ACT.Exp, scale=-1.0, bias=least[b][:],
                 accum_out=total[b][:],
             )
 

from contextlib import ExitStack

import concourse.mybir as mybir
from concourse.masks import make_identity

K, T, S, H, V, W = 512, 1024, 512, 512, 512, 2048
P = 128
PACK = 4
BLOCKS = S // P
SCALAR_SHARE = 80
ROW0 = P - 2 * BLOCKS

FLOPS = 2 * K * H * S + 2 * H * S * V
BYTES = K * T + 16 * T + 4 * K * H + H * W + 16 * W + 8 * S + 4 * W + 2 * 2 * P * 32 + 4 * S * V

F32 = mybir.dt.float32
BF16 = mybir.dt.bfloat16
I32 = mybir.dt.int32
U32 = mybir.dt.uint32
U16 = mybir.dt.uint16
U8 = mybir.dt.uint8
FP8X4 = mybir.dt.float8_e4m3fn_x4
ALU = mybir.AluOpType
ACT = mybir.ActivationFunctionType
AXIS = mybir.AxisListType


def tile_picked_yscann_soft_p_kernel(
    tc, x_words, x_scales, w1, e_words, e_scales, own, inv, qn, offs, code, out
):
    nc = tc.nc
    with ExitStack() as ctx:
        keep = ctx.enter_context(tc.tile_pool(name="keep", bufs=1))
        psum = ctx.enter_context(tc.psum_pool(name="psum", bufs=1))

        offs_sb = keep.tile([P, S // 16], U16, name="offs_sb")
        code_sb = keep.tile([P, V // 16], U16, name="code_sb")
        xw_all = keep.tile([P, T], I32, name="xw_all")
        xs_all = keep.tile([P, T], U8, name="xs_all", tag="e_words", align_bytes=64)
        ew_all = keep.tile([P, W], I32, name="ew_all", tag="e_words", align_bytes=64)
        es_all = keep.tile([P, W], U8, name="es_all", tag="e_scales", align_bytes=64)
        q_all = keep.tile([P, W], F32, name="q_all", tag="norms", align_bytes=64)
        w_raw = keep.tile([P, PACK, H], F32, name="w_raw")
        rows = keep.tile([P, P], F32, name="rows")
        ident = keep.tile([P, P], F32, name="ident")
        warm = keep.tile([P, 1], F32, name="warm")

        nc.vector.memset(q_all[: P - 1, :], 0.0)
        nc.gpsimd.memset(rows[:ROW0, :], 0.0)
        nc.scalar.activation(out=warm[:32, :], in_=rows[:32, 0:1], func=ACT.Exp)

        def load_scales(tile, scales):
            for q in range(4):
                nc.sync.dma_start(
                    out=tile[32 * q : 32 * q + 32, :].bitcast(I32),
                    in_=scales[0, 4 * q : 4 * q + 4, :].bitcast(I32).partition_broadcast(8),
                )

        w_view = w1.rearrange("(p j) c -> p j c", j=PACK)
        nc.gpsimd.dma_start(out=rows[ROW0 : ROW0 + BLOCKS, :], in_=own.rearrange("(b p) o -> b (p o)", p=P))
        nc.gpsimd.dma_start(out=rows[ROW0 + BLOCKS :, :], in_=inv.rearrange("(b p) o -> b (p o)", p=P))
        make_identity(nc, ident[:])
        nc.sync.dma_start(offs_sb[:], offs)
        nc.sync.dma_start(code_sb[:], code)
        load_scales(xs_all, x_scales)
        nc.sync.dma_start(out=xw_all[:], in_=x_words[0].rearrange("p n t -> p (n t)").bitcast(I32))
        nc.sync.dma_start(out=w_raw[:], in_=w_view)
        nc.sync.dma_start(out=q_all[P - 1 :, :], in_=qn[0:1, :])
        load_scales(es_all, e_scales)
        nc.sync.dma_start(out=ew_all[:], in_=e_words[0].rearrange("p n t -> p (n t)").bitcast(I32))

        xw = keep.tile([P, S], U32, name="xw", align_bytes=64)
        xs = keep.tile([P, S], U8, name="xs", align_bytes=64)
        ew = keep.tile([P, V], U32, name="ew", tag="e_scales", align_bytes=64)
        es = keep.tile([P, V], U8, name="es", tag="w_bf", align_bytes=64)
        q_row = keep.tile([P, V], F32, name="q_row")

        nc.vector.tensor_copy(xs[:], xs_all[:].indirect(offs_sb[:]))
        nc.vector.tensor_copy(xw[:], xw_all[:].bitcast(U32).indirect(offs_sb[:]))
        nc.vector.tensor_copy(q_row[:], q_all[:].indirect(code_sb[:]))

        turn = psum.tile([P, PACK, P], F32, name="turn", tag="z3")
        nc.tensor.transpose(turn[:, 0, :], rows[:], ident[:])
        own_s = keep.tile([P, BLOCKS], F32, name="own_s")
        inv_a = keep.tile([P, BLOCKS], F32, name="inv_a")
        inv_b = keep.tile([P, BLOCKS], F32, name="inv_b")
        nc.scalar.activation(out=own_s[:], in_=turn[:, 0, ROW0 : ROW0 + BLOCKS], func=ACT.Copy, scale=-1.25)
        nc.scalar.activation(out=inv_a[:], in_=turn[:, 0, ROW0 + BLOCKS :], func=ACT.Copy, scale=-0.8)
        nc.scalar.activation(out=inv_b[:], in_=turn[:, 0, ROW0 + BLOCKS :], func=ACT.Copy, scale=-1.6)

        w_bf = keep.tile([P, PACK * H], BF16, name="w_bf", tag="w_bf", align_bytes=64)
        w_dst = w_bf[:].rearrange("p (t m j) -> p m j t", t=PACK, j=PACK)
        w_src = w_raw[:].rearrange("p j (m t) -> p m j t", t=PACK)
        nc.scalar.copy(out=w_dst[:, :SCALAR_SHARE], in_=w_src[:, :SCALAR_SHARE])
        nc.vector.tensor_copy(out=w_dst[:, SCALAR_SHARE:], in_=w_src[:, SCALAR_SHARE:])
        wq = keep.tile([P, H], U32, name="wq", tag="norms", align_bytes=64)
        ws = keep.tile([P, H], U8, name="ws", align_bytes=64)
        nc.vector.quantize_mx(out=wq[:].bitcast(FP8X4), scales=ws[:], in_=w_bf[:])
        nc.vector.tensor_copy(es[:], es_all[:].indirect(code_sb[:]))
        nc.vector.tensor_copy(ew[:], ew_all[:].bitcast(U32).indirect(code_sb[:]))

        turn_q = psum.tile([P, PACK, P], F32, name="turn_q", tag="z2")
        for c in range(PACK):
            nc.tensor.transpose(turn_q[:, c, :], q_row[:, c * P : (c + 1) * P], ident[:])
        q_col = keep.tile([P, PACK], F32, name="q_col")
        nc.scalar.copy(out=q_col[:], in_=turn_q[:, :, P - 1])
        q_bank = psum.tile([P, V], F32, name="q_bank", tag="z1")
        for c in range(PACK):
            nc.tensor.transpose(
                q_bank[:, c * P : (c + 1) * P], q_col[:, c : c + 1].to_broadcast([P, P]), ident[:]
            )
        q_s = keep.tile([P, V], F32, name="q_s")
        nc.scalar.activation(out=q_s[:], in_=q_bank[:], func=ACT.Copy, scale=-1.25)

        hq_all = keep.tile([P, S], U32, name="hq_all", tag="e_words", align_bytes=64)
        hq = []
        hs = []
        for b in range(BLOCKS):
            cols = slice(b * P, (b + 1) * P)
            h_bank = psum.tile([P, PACK, P], F32, name="h_bank", tag="h_bank", bufs=4)
            for t in range(PACK):
                nc.tensor.matmul_mx(
                    out=h_bank[:, t, :],
                    lhsT=wq[:, t * P : (t + 1) * P].bitcast(FP8X4),
                    lhsT_scale=ws[:, t * P : (t + 1) * P],
                    rhs=xw[:, cols].bitcast(FP8X4),
                    rhs_scale=xs[:, cols],
                    start=True,
                    stop=True,
                )
            h_bf = keep.tile([P, P, PACK], BF16, name=f"h_bf{b}", align_bytes=64)
            nc.scalar.copy(out=h_bf[:], in_=h_bank[:].rearrange("p t n -> p n t"))
            hq_b = hq_all[:, cols]
            hs_b = keep.tile([P, P], U8, name=f"hs{b}", align_bytes=64)
            nc.vector.quantize_mx(
                out=hq_b.bitcast(FP8X4), scales=hs_b[:], in_=h_bf[:].rearrange("p n t -> p (n t)")
            )
            hq.append(hq_b)
            hs.append(hs_b)

        def stage_tiles(name, width):
            return [keep.tile([P, width], F32, name=f"{name}{b}") for b in range(BLOCKS)]

        tot2, rr_sq, big2, cost2, ex, res = (
            stage_tiles(n, V) for n in ("tot2", "rr_sq", "big2", "cost2", "ex", "res")
        )
        least, total, share = (stage_tiles(n, 1) for n in ("least", "total", "share"))
        z = [psum.tile([P, V], F32, name=f"z{b}", tag=f"z{b}") for b in range(BLOCKS)]

        def product(b):
            nc.tensor.matmul_mx(
                out=z[b][:],
                lhsT=hq[b].bitcast(FP8X4),
                lhsT_scale=hs[b][:],
                rhs=ew[:].bitcast(FP8X4),
                rhs_scale=es[:],
                start=True,
                stop=True,
            )

        def read_bank(b):
            nc.vector.scalar_tensor_tensor(
                out=tot2[b][:], in0=z[b][:], scalar=own_s[:, b : b + 1], in1=q_s[:], op0=ALU.add, op1=ALU.add
            )
            nc.scalar.activation(
                out=rr_sq[b][:], in_=z[b][:], func=ACT.Square, scale=0.5, bias=own_s[:, b : b + 1]
            )


        def larger(b):
            nc.vector.scalar_tensor_tensor(
                out=big2[b][:], in0=rr_sq[b][:], scalar=inv_a[:, b : b + 1], in1=tot2[b][:],
                op0=ALU.mult, op1=ALU.min,
            )

        def cost(b):
            nc.vector.scalar_tensor_tensor(
                out=cost2[b][:], in0=rr_sq[b][:], scalar=inv_b[:, b : b + 1], in1=big2[b][:],
                op0=ALU.mult, op1=ALU.add,
            )

        def smallest(b):
            nc.vector.tensor_scalar(
                out=big2[b][:], in0=cost2[b][:], scalar1=-1.6, scalar2=None, op0=ALU.mult, op1=ALU.min,
                accum_out=least[b][:],
            )
            nc.scalar.activation(
                out=ex[b][:], in_=big2[b][:], func=ACT.Exp, scale=-1.0, bias=least[b][:],
                accum_out=total[b][:],
            )

        def finish(b):
            nc.vector.reciprocal(out=share[b][:], in_=total[b][:])
            if b < BLOCKS - 1:
                nc.scalar.activation(out=res[b][:], in_=ex[b][:], func=ACT.Copy, scale=share[b][:])
            else:
                nc.vector.tensor_scalar(
                    out=res[b][:], in0=ex[b][:], scalar1=share[b][:], scalar2=None, op0=ALU.mult
                )
            nc.sync.dma_start(out=out[b * P : (b + 1) * P, :], in_=res[b][:])

        for b in range(BLOCKS):
            product(b)
        stages = (read_bank, larger, cost, smallest, finish)
        for step in range(BLOCKS + len(stages) - 1):
            for k in reversed(range(len(stages))):
                if 0 <= step - k < BLOCKS:
                    stages[k](step - k)
